import numpy as np
import ml_dtypes


def mxq(x, axis, fmt="e4m3"):
    dtype, down = {"e4m3": (ml_dtypes.float8_e4m3fn, 7), "e5m2": (ml_dtypes.float8_e5m2, 14)}[fmt]
    v = np.moveaxis(np.asarray(x, np.float32).astype(ml_dtypes.bfloat16).astype(np.float64), axis, -1)
    blocks = v.reshape(v.shape[:-1] + (-1, 32))
    amax = np.abs(blocks).max(-1, keepdims=True)
    byte = np.maximum(np.where(amax > 0, np.frexp(amax)[1] - 1 + 127, 0) - down, 1)
    scale = np.exp2(byte - 127.0)
    codes = (blocks / scale).astype(np.float32).astype(dtype).astype(np.float64)
    return np.moveaxis((codes * scale).reshape(v.shape), -1, axis)


WIDE = False


def mx_kscale(k):
    if not WIDE:
        return np.ones(k)
    levels = np.array([10, -10, 5, -5, 0])
    if k % 512:
        return np.exp2(np.random.permutation(np.resize(levels, k // 32))).repeat(32)
    a = np.empty((k // 512, 16))
    for p in range(k // 512):
        a[p, :8] = np.random.permutation(np.resize(levels, 8))
        for g in range(8):
            far = levels[np.abs(levels - a[p, g]) >= 10]
            a[p, g + 8] = far[np.random.randint(len(far))]
    return np.exp2(a.ravel()).repeat(32)


def f64(x):
    return np.asarray(x).astype(np.float64)


def striped(idx):
    return np.tile(idx.reshape(-1, 16).T, (8, 1)).astype(np.uint16)


def unstriped(offs):
    return offs[:16].T.reshape(-1).astype(np.int64)


def striped8(idx):
    return np.concatenate([x.reshape(-1, 16).T for x in idx]).astype(np.uint16)


def runs(offs, k):
    lists = np.stack([offs[16 * r : 16 * r + 16].T.reshape(-1) for r in range(8)]).astype(np.int64)
    return lists[np.arange(k) % 512 // 64]


def pack_weight(w):
    k, n = w.shape
    w = f64(np.asarray(w, np.float32).astype(ml_dtypes.bfloat16)).reshape(k // 32, 32, n)
    amax = np.abs(w).max(1)
    byte = np.clip(np.where(amax > 0, np.frexp(amax)[1] - 1 + 127 - 7, 1), 1, 254)
    scaled = (w * np.exp2(127.0 - byte)[:, None, :]).reshape(k, n).astype(np.float32)
    words = np.ascontiguousarray(scaled.reshape(k // 512, 128, 4, n).transpose(0, 1, 3, 2)).astype(ml_dtypes.float8_e4m3fn).view(np.uint8)
    return words, np.ascontiguousarray(byte.astype(np.uint8).reshape(k // 512, 16, n))


def unpack_weight(words, scales):
    g, p, n, _ = words.shape
    vals = np.ascontiguousarray(words).view(ml_dtypes.float8_e4m3fn).astype(np.float64) * np.repeat(np.exp2(scales.astype(np.float64) - 127.0), 8, axis=1)[..., None]
    return vals.transpose(0, 1, 3, 2).reshape(g * 512, n)

def planes(y):
    n, m = y.shape
    v = y.astype(np.float32).astype(ml_dtypes.bfloat16).astype(np.float64).reshape(n // 32, 32, m)
    top = np.abs(v).max(1)
    byte = np.clip(np.where(top > 0, np.frexp(top)[1] - 1 + 127 - 7, 1), 1, 254)
    codes = (v * np.exp2(127.0 - byte)[:, None, :]).reshape(n, m).astype(np.float32).astype(ml_dtypes.float8_e4m3fn).view(np.uint8)
    words = codes.reshape(n // 512, 128, 4, m).transpose(0, 1, 3, 2)
    return np.ascontiguousarray(words), np.ascontiguousarray(byte.astype(np.uint8).reshape(n // 512, 16, m))


K, T, S, N, W = 512, 2048, 512, 512, 256


def setup_inputs():
    n = np.random.standard_normal
    s = mx_kscale(K)[:, None]
    packed_xT = pack_weight(n((K, T)) * s)
    perm = np.stack([np.random.permutation(S) for _ in range(8)])
    return {
        "x_words": packed_xT[0],
        "x_scales": packed_xT[1],
        "w1": (n((K, N)) / np.sqrt(2 * K) / s).astype(np.float32),
        "w2": (n((K, N)) / np.sqrt(2 * K) / s).astype(np.float32),
        "offs": striped(np.random.permutation(T)[:S]),
        "two": striped(np.random.permutation(T)[:S]),
        "n1": striped8(perm[:, :W]),
        "n2": striped8(perm[:, W:]),
        "n3": striped8(np.stack([np.random.permutation(S) for _ in range(8)])),
    }


def reference(x_words, x_scales, w1, w2, offs, two, n1, n2, n3):
    xq = unpack_weight(x_words, x_scales)[:, unstriped(offs)]
    x_two = unpack_weight(x_words, x_scales)[:, unstriped(two)]
    h = mxq(f64(w1), 0, "e4m3").T @ xq + mxq(f64(w2), 0, "e4m3").T @ x_two
    pa = h[np.arange(N)[:, None], runs(n1, N)]
    pb = h[np.arange(N)[:, None], runs(n2, N)]
    rb = pa - pb
    ds = np.zeros((N, S))
    ds[np.arange(N)[:, None], runs(n1, N)] = pb
    dt = ds.copy()
    dt[np.arange(N)[:, None], runs(n2, N)] = rb
    out_0 = np.maximum(dt, 0.5 * (dt[np.arange(N)[:, None], runs(n3, N)]))
    return (out_0,) + planes(out_0)

@@ -1,0 +1,172 @@
+from contextlib import ExitStack
+
+import concourse.mybir as mybir
+
+F32 = mybir.dt.float32
+BF16 = mybir.dt.bfloat16
+I32 = mybir.dt.int32
+U32 = mybir.dt.uint32
+U16 = mybir.dt.uint16
+U8 = mybir.dt.uint8
+FP8X4 = mybir.dt.float8_e4m3fn_x4
+ALU = mybir.AluOpType
+COPY = mybir.ActivationFunctionType.Copy
+
+P = 128
+PACK = 4
+K, T, S, N, W = 512, 2048, 512, 512, 256
+FLOPS = 2 * 2 * K * N * S
+
+
+def tile_picked_ottswapd_none_po_kernel(
+    tc, x_words, x_scales, w1, w2, offs, two, n1, n2, n3, out_0, out_1, out_2
+):
+    nc = tc.nc
+    with ExitStack() as ctx:
+        sb = ctx.enter_context(tc.tile_pool(name="sb", bufs=1))
+        ps = ctx.enter_context(tc.psum_pool(name="ps", bufs=1))
+
+        def load_list(src, name):
+            tile = sb.tile(list(src.shape), U16, name=name)
+            nc.sync.dma_start(tile[:], src)
+            return tile
+
+        xs = sb.tile([P, T], U8, name="xs", align_bytes=64)
+        nc.vector.memset(xs[:].bitcast(I32), 0)
+        for q in range(4):
+            nc.scalar.dma_start(xs[32 * q : 32 * q + 4, :].bitcast(I32), x_scales[0, 4 * q : 4 * q + 4, :].bitcast(I32))
+        pick = [load_list(offs, "l_offs"), load_list(two, "l_two")]
+        raw = [sb.tile([P, PACK, N], F32, name=f"raw{i}", align_bytes=64) for i in range(2)]
+        xw = sb.tile([P, T], U32, name="xw", align_bytes=64)
+        nc.sync.dma_start(raw[0][:], w1.rearrange("(p j) c -> p j c", j=PACK))
+        nc.sync.dma_start(xw[:].bitcast(I32), x_words[0].rearrange("p n t -> p (n t)").bitcast(I32))
+        nc.sync.dma_start(raw[1][:], w2.rearrange("(p j) c -> p j c", j=PACK))
+        l1, l2, l3 = load_list(n1, "l_n1"), load_list(n2, "l_n2"), load_list(n3, "l_n3")
+        minus = sb.tile([P, W], F32, name="minus", align_bytes=64)
+        nc.gpsimd.memset(minus[:], -1.0)
+
+        gs = [sb.tile([P, S], U8, name=f"gs{i}", align_bytes=64) for i in range(2)]
+        gw = [sb.tile([P, S], U32, name=f"gw{i}", align_bytes=64) for i in range(2)]
+        for i in range(2):
+            nc.vector.tensor_copy(gs[i][:], xs[:].indirect(pick[i][:]))
+
+        wb = [sb.tile([P, PACK * N], BF16, name=f"wb{i}", align_bytes=64) for i in range(2)]
+        wq = [sb.tile([P, N], U32, name=f"wq{i}", align_bytes=64) for i in range(2)]
+        wsc = [sb.tile([P, N], U8, name=f"wsc{i}", align_bytes=64) for i in range(2)]
+
+        def deal(i, ms, ts, on_scalar):
+            dst = wb[i][:].rearrange("p (t m j) -> p m j t", t=PACK, j=PACK)[:, ms, :, ts]
+            src = raw[i][:].rearrange("p j (m t) -> p m j t", t=PACK)[:, ms, :, ts]
+            if on_scalar:
+                nc.scalar.activation(dst, src, COPY)
+            else:
+                nc.vector.tensor_copy(dst, src)
+
+        def quantise_w(i, c0, c1):
+            nc.vector.quantize_mx(
+                out=wq[i][:, c0:c1].bitcast(FP8X4), scales=wsc[i][:, c0:c1], in_=wb[i][:, PACK * c0 : PACK * c1]
+            )
+
+        for u in range(2):
+            deal(0, slice(0, P), slice(2 * u, 2 * u + 2), True)
+            quantise_w(0, 2 * u * P, (2 * u + 2) * P)
+        for i in range(2):
+            nc.vector.tensor_copy(gw[i][:], xw[:].indirect(pick[i][:]))
+        deal(1, slice(0, 40), slice(0, 2), True)
+        deal(1, slice(40, P), slice(0, 2), False)
+        quantise_w(1, 0, P)
+        quantise_w(1, P, 2 * P)
+        deal(1, slice(0, 40), slice(2, 4), True)
+        deal(1, slice(40, P), slice(2, 4), False)
+        quantise_w(1, 2 * P, N)
+
+        halves = [slice(0, W), slice(W, S)]
+        spans = [halves] + [[slice(0, S)]] * (PACK - 1)
+        acc = [
+            [ps.tile([P, c.stop - c.start], F32, name=f"acc{t}_{c.start}") for c in spans[t]] for t in range(PACK)
+        ]
+        for t in range(PACK):
+            cols = slice(t * P, (t + 1) * P)
+            for bank, c in zip(acc[t], spans[t]):
+                for i in range(2):
+                    nc.tensor.matmul_mx(
+                        out=bank[:],
+                        lhsT=wq[i][:, cols].bitcast(FP8X4),
+                        lhsT_scale=wsc[i][:, cols],
+                        rhs=gw[i][:, c].bitcast(FP8X4),
+                        rhs_scale=gs[i][:, c],
+                        start=(i == 0),
+                        stop=(i == 1),
+                    )
+
+        h = [sb.tile([P, S], F32, name=f"h{t}", align_bytes=64) for t in range(PACK)]
+        pa = [sb.tile([P, W], F32, name=f"pa{t}", align_bytes=64) for t in range(PACK)]
+        npb = [sb.tile([P, W], F32, name=f"npb{t}", align_bytes=64) for t in range(PACK)]
+        dt = [sb.tile([P, S], F32, name=f"dt{t}", align_bytes=64) for t in range(PACK)]
+        far = [sb.tile([P, S], F32, name=f"far{t}", align_bytes=64) for t in range(PACK)]
+        y = [sb.tile([P, 2, S], F32, name=f"y{u}", align_bytes=64) for u in range(2)]
+        yb = sb.tile([P, S, PACK], BF16, name="yb", align_bytes=64)
+        yq = sb.tile([P, S], U32, name="yq", align_bytes=64)
+        ysc = sb.tile([P, S], U8, name="ysc", align_bytes=64)
+        out_rows = out_0.rearrange("(p t) c -> p t c", t=PACK)
+        out_words = out_1[0].rearrange("p c r -> p (c r)").bitcast(I32)
+
+        def put_pb(t):
+            nc.scalar.activation(h[t][:, spans[t][0]], acc[t][0][:], COPY)
+            if t == 0:
+                nc.vector.tensor_copy(h[t][:, spans[t][1]], acc[t][1][:])
+            nc.scalar.activation(npb[t][:], h[t][:].indirect(l2[:]), COPY, scale=-1.0)
+            nc.vector.tensor_tensor(dt[t][:].indirect(l1[:]), npb[t][:], minus[:], ALU.mult)
+
+        def put_rb(t):
+            nc.scalar.activation(pa[t][:], h[t][:].indirect(l1[:]), COPY)
+            nc.vector.tensor_tensor(dt[t][:].indirect(l2[:]), pa[t][:], npb[t][:], ALU.add)
+
+        def look(t, c):
+            nc.scalar.activation(far[t][:, c], dt[t][:].indirect(l3[:, c.start // 16 : c.stop // 16]), COPY)
+
+        def larger(t, c):
+            dst = y[t // 2][:, t % 2, c]
+            nc.vector.scalar_tensor_tensor(dst, far[t][:, c], 0.5, dt[t][:, c], ALU.mult, ALU.max)
+            nc.sync.dma_start(out_rows[:, t, c], dst)
+
+        def round_pair(u, c, on_scalar):
+            dst = yb[:, c, 2 * u : 2 * u + 2]
+            src = y[u][:, :, c].rearrange("p t c -> p c t")
+            if on_scalar:
+                nc.scalar.activation(dst, src, COPY)
+            else:
+                nc.vector.tensor_copy(dst, src)
+
+        def quantise_y(c):
+            nc.vector.quantize_mx(
+                out=yq[:, c].bitcast(FP8X4), scales=ysc[:, c], in_=yb[:, c, :].rearrange("p c t -> p (c t)")
+            )
+            nc.sync.dma_start(out_words[:, c], yq[:, c].bitcast(I32))
+
+        def finish(t):
+            for c in halves:
+                look(t, c)
+            larger(t, slice(0, S))
+
+        put_pb(0)
+        put_pb(1)
+        put_rb(0)
+        put_rb(1)
+        for t in (2, 3):
+            put_pb(t)
+            finish(t - 2)
+            put_rb(t)
+        finish(2)
+        round_pair(0, slice(0, S), True)
+        for c in halves:
+            look(PACK - 1, c)
+        for c in halves:
+            larger(PACK - 1, c)
+        round_pair(1, halves[0], True)
+        round_pair(1, halves[1], False)
+        for c in halves:
+            quantise_y(c)
+        for q in range(4):
+            eng = nc.scalar if q % 2 else nc.sync
+            eng.dma_start(out_2[0, 4 * q : 4 * q + 4, :].bitcast(I32), ysc[32 * q : 32 * q + 4, :].bitcast(I32))

@@ -31,15 +31,17 @@ def tile_picked_ottswapd_none_po_kernel(
             nc.sync.dma_start(tile[:], src)
             return tile
 
+        pick = [load_list(offs, "l_offs"), load_list(two, "l_two")]
         xs = sb.tile([P, T], U8, name="xs", align_bytes=64)
         nc.vector.memset(xs[:].bitcast(I32), 0)
-        for q in range(4):
-            nc.scalar.dma_start(xs[32 * q : 32 * q + 4, :].bitcast(I32), x_scales[0, 4 * q : 4 * q + 4, :].bitcast(I32))
-        pick = [load_list(offs, "l_offs"), load_list(two, "l_two")]
         raw = [sb.tile([P, PACK, N], F32, name=f"raw{i}", align_bytes=64) for i in range(2)]
         xw = sb.tile([P, T], U32, name="xw", align_bytes=64)
+        words = x_words[0].rearrange("p n t -> p (n t)").bitcast(I32)
+        nc.sync.dma_start(xw[:, : T // 2].bitcast(I32), words[:, : T // 2])
+        for q in range(4):
+            nc.sync.dma_start(xs[32 * q : 32 * q + 4, :].bitcast(I32), x_scales[0, 4 * q : 4 * q + 4, :].bitcast(I32))
+        nc.sync.dma_start(xw[:, T // 2 :].bitcast(I32), words[:, T // 2 :])
         nc.sync.dma_start(raw[0][:], w1.rearrange("(p j) c -> p j c", j=PACK))
-        nc.sync.dma_start(xw[:].bitcast(I32), x_words[0].rearrange("p n t -> p (n t)").bitcast(I32))
         nc.sync.dma_start(raw[1][:], w2.rearrange("(p j) c -> p j c", j=PACK))
         l1, l2, l3 = load_list(n1, "l_n1"), load_list(n2, "l_n2"), load_list(n3, "l_n3")
         minus = sb.tile([P, W], F32, name="minus", align_bytes=64)
@@ -50,44 +52,46 @@ def tile_picked_ottswapd_none_po_kernel(
         for i in range(2):
             nc.vector.tensor_copy(gs[i][:], xs[:].indirect(pick[i][:]))
 
-        wb = [sb.tile([P, PACK * N], BF16, name=f"wb{i}", align_bytes=64) for i in range(2)]
         wq = [sb.tile([P, N], U32, name=f"wq{i}", align_bytes=64) for i in range(2)]
         wsc = [sb.tile([P, N], U8, name=f"wsc{i}", align_bytes=64) for i in range(2)]
 
-        def deal(i, ms, ts, on_scalar):
-            dst = wb[i][:].rearrange("p (t m j) -> p m j t", t=PACK, j=PACK)[:, ms, :, ts]
-            src = raw[i][:].rearrange("p j (m t) -> p m j t", t=PACK)[:, ms, :, ts]
+        def deal(i, u, tag, on_scalar):
+            stage = sb.tile([P, 2 * P * PACK], BF16, name=f"wb{i}{u}", tag=tag, align_bytes=64)
+            dst = stage[:].rearrange("p (t m j) -> p m j t", t=2, j=PACK)
+            src = raw[i][:].rearrange("p j (m t) -> p m j t", t=PACK)[:, :, :, 2 * u : 2 * u + 2]
             if on_scalar:
                 nc.scalar.activation(dst, src, COPY)
             else:
                 nc.vector.tensor_copy(dst, src)
+            return stage
 
-        def quantise_w(i, c0, c1):
+        def quantise_w(i, u, stage, c0, c1):
+            cols = slice(2 * P * u + c0, 2 * P * u + c1)
             nc.vector.quantize_mx(
-                out=wq[i][:, c0:c1].bitcast(FP8X4), scales=wsc[i][:, c0:c1], in_=wb[i][:, PACK * c0 : PACK * c1]
+                out=wq[i][:, cols].bitcast(FP8X4), scales=wsc[i][:, cols], in_=stage[:, PACK * c0 : PACK * c1]
             )
 
-        for u in range(2):
-            deal(0, slice(0, P), slice(2 * u, 2 * u + 2), True)
-            quantise_w(0, 2 * u * P, (2 * u + 2) * P)
         for i in range(2):
             nc.vector.tensor_copy(gw[i][:], xw[:].indirect(pick[i][:]))
-        deal(1, slice(0, 40), slice(0, 2), True)
-        deal(1, slice(40, P), slice(0, 2), False)
-        quantise_w(1, 0, P)
-        quantise_w(1, P, 2 * P)
-        deal(1, slice(0, 40), slice(2, 4), True)
-        deal(1, slice(40, P), slice(2, 4), False)
-        quantise_w(1, 2 * P, N)
+        quantise_w(0, 0, deal(0, 0, "first", True), 0, 2 * P)
+        late = deal(0, 1, "second", True)
+        stage = deal(1, 0, "first", False)
+        quantise_w(1, 0, stage, 0, P)
+        quantise_w(1, 0, stage, P, 2 * P)
+        quantise_w(0, 1, late, 0, 2 * P)
+        quantise_w(1, 1, deal(1, 1, "first", False), 0, 2 * P)
 
         halves = [slice(0, W), slice(W, S)]
         spans = [halves] + [[slice(0, S)]] * (PACK - 1)
-        acc = [
-            [ps.tile([P, c.stop - c.start], F32, name=f"acc{t}_{c.start}") for c in spans[t]] for t in range(PACK)
-        ]
-        for t in range(PACK):
+        bank_tags = [["bank0", "bank1"], ["bank2"], ["bank0"], ["bank1"]]
+        acc = []
+
+        def multiply(t):
             cols = slice(t * P, (t + 1) * P)
-            for bank, c in zip(acc[t], spans[t]):
+            banks = []
+            for tag, c in zip(bank_tags[t], spans[t]):
+                bank = ps.tile([P, c.stop - c.start], F32, name=f"acc{t}_{c.start}", tag=tag)
+                banks.append(bank)
                 for i in range(2):
                     nc.tensor.matmul_mx(
                         out=bank[:],
@@ -98,13 +102,14 @@ def tile_picked_ottswapd_none_po_kernel(
                         start=(i == 0),
                         stop=(i == 1),
                     )
+            acc.append(banks)
 
         h = [sb.tile([P, S], F32, name=f"h{t}", align_bytes=64) for t in range(PACK)]
         pa = [sb.tile([P, W], F32, name=f"pa{t}", align_bytes=64) for t in range(PACK)]
         npb = [sb.tile([P, W], F32, name=f"npb{t}", align_bytes=64) for t in range(PACK)]
         dt = [sb.tile([P, S], F32, name=f"dt{t}", align_bytes=64) for t in range(PACK)]
         far = [sb.tile([P, S], F32, name=f"far{t}", align_bytes=64) for t in range(PACK)]
-        y = [sb.tile([P, 2, S], F32, name=f"y{u}", align_bytes=64) for u in range(2)]
+        y = sb.tile([P, PACK, S], F32, name="y", align_bytes=64)
         yb = sb.tile([P, S, PACK], BF16, name="yb", align_bytes=64)
         yq = sb.tile([P, S], U32, name="yq", align_bytes=64)
         ysc = sb.tile([P, S], U8, name="ysc", align_bytes=64)
@@ -112,9 +117,9 @@ def tile_picked_ottswapd_none_po_kernel(
         out_words = out_1[0].rearrange("p c r -> p (c r)").bitcast(I32)
 
         def put_pb(t):
-            nc.scalar.activation(h[t][:, spans[t][0]], acc[t][0][:], COPY)
-            if t == 0:
-                nc.vector.tensor_copy(h[t][:, spans[t][1]], acc[t][1][:])
+            multiply(t)
+            for bank, c in zip(acc[t], spans[t]):
+                nc.scalar.activation(h[t][:, c], bank[:], COPY)
             nc.scalar.activation(npb[t][:], h[t][:].indirect(l2[:]), COPY, scale=-1.0)
             nc.vector.tensor_tensor(dt[t][:].indirect(l1[:]), npb[t][:], minus[:], ALU.mult)
 
@@ -126,13 +131,13 @@ def tile_picked_ottswapd_none_po_kernel(
             nc.scalar.activation(far[t][:, c], dt[t][:].indirect(l3[:, c.start // 16 : c.stop // 16]), COPY)
 
         def larger(t, c):
-            dst = y[t // 2][:, t % 2, c]
+            dst = y[:, t, c]
             nc.vector.scalar_tensor_tensor(dst, far[t][:, c], 0.5, dt[t][:, c], ALU.mult, ALU.max)
             nc.sync.dma_start(out_rows[:, t, c], dst)
 
-        def round_pair(u, c, on_scalar):
-            dst = yb[:, c, 2 * u : 2 * u + 2]
-            src = y[u][:, :, c].rearrange("p t c -> p c t")
+        def round_y(c, on_scalar):
+            dst = yb[:, c, :]
+            src = y[:, :, c].rearrange("p t c -> p c t")
             if on_scalar:
                 nc.scalar.activation(dst, src, COPY)
             else:
@@ -158,15 +163,16 @@ def tile_picked_ottswapd_none_po_kernel(
             finish(t - 2)
             put_rb(t)
         finish(2)
-        round_pair(0, slice(0, S), True)
         for c in halves:
             look(PACK - 1, c)
-        for c in halves:
-            larger(PACK - 1, c)
-        round_pair(1, halves[0], True)
-        round_pair(1, halves[1], False)
-        for c in halves:
-            quantise_y(c)
+        larger(PACK - 1, halves[0])
+        round_y(slice(64, W), False)
+        round_y(slice(0, 64), True)
+        larger(PACK - 1, halves[1])
+        quantise_y(halves[0])
+        round_y(slice(W, W + 96), True)
+        round_y(slice(W + 96, S), False)
+        quantise_y(halves[1])
         for q in range(4):
             eng = nc.scalar if q % 2 else nc.sync
             eng.dma_start(out_2[0, 4 * q : 4 * q + 4, :].bitcast(I32), ysc[32 * q : 32 * q + 4, :].bitcast(I32))

@@ -79,7 +79,7 @@ def tile_picked_ottswapd_none_po_kernel(
         quantise_w(1, 0, stage, 0, P)
         quantise_w(1, 0, stage, P, 2 * P)
         quantise_w(0, 1, late, 0, 2 * P)
-        quantise_w(1, 1, deal(1, 1, "first", False), 0, 2 * P)
+        quantise_w(1, 1, deal(1, 1, "third", True), 0, 2 * P)
 
         halves = [slice(0, W), slice(W, S)]
         spans = [halves] + [[slice(0, S)]] * (PACK - 1)
@@ -136,8 +136,8 @@ def tile_picked_ottswapd_none_po_kernel(
             nc.sync.dma_start(out_rows[:, t, c], dst)
 
         def round_y(c, on_scalar):
-            dst = yb[:, c, :]
-            src = y[:, :, c].rearrange("p t c -> p c t")
+            dst = yb[:, c, :].rearrange("p (c i) t -> p c t i", i=4)
+            src = y[:, :, c].rearrange("p t (c i) -> p c t i", i=4)
             if on_scalar:
                 nc.scalar.activation(dst, src, COPY)
             else:

from contextlib import ExitStack

import concourse.mybir as mybir

F32 = mybir.dt.float32
BF16 = mybir.dt.bfloat16
I32 = mybir.dt.int32
U32 = mybir.dt.uint32
U16 = mybir.dt.uint16
U8 = mybir.dt.uint8
FP8X4 = mybir.dt.float8_e4m3fn_x4
ALU = mybir.AluOpType
COPY = mybir.ActivationFunctionType.Copy

P = 128
PACK = 4
K, T, S, N, W = 512, 2048, 512, 512, 256
FLOPS = 2 * 2 * K * N * S


def tile_picked_ottswapd_none_po_kernel(
    tc, x_words, x_scales, w1, w2, offs, two, n1, n2, n3, out_0, out_1, out_2
):
    nc = tc.nc
    with ExitStack() as ctx:
        sb = ctx.enter_context(tc.tile_pool(name="sb", bufs=1))
        ps = ctx.enter_context(tc.psum_pool(name="ps", bufs=1))

        def load_list(src, name):
            tile = sb.tile(list(src.shape), U16, name=name)
            nc.sync.dma_start(tile[:], src)
            return tile

        pick = [load_list(offs, "l_offs"), load_list(two, "l_two")]
        xs = sb.tile([P, T], U8, name="xs", align_bytes=64)
        nc.vector.memset(xs[:].bitcast(I32), 0)
        raw = [sb.tile([P, PACK, N], F32, name=f"raw{i}", align_bytes=64) for i in range(2)]
        xw = sb.tile([P, T], U32, name="xw", align_bytes=64)
        words = x_words[0].rearrange("p n t -> p (n t)").bitcast(I32)
        nc.sync.dma_start(xw[:, : T // 2].bitcast(I32), words[:, : T // 2])
        for q in range(4):
            nc.sync.dma_start(xs[32 * q : 32 * q + 4, :].bitcast(I32), x_scales[0, 4 * q : 4 * q + 4, :].bitcast(I32))
        nc.sync.dma_start(xw[:, T // 2 :].bitcast(I32), words[:, T // 2 :])
        nc.sync.dma_start(raw[0][:], w1.rearrange("(p j) c -> p j c", j=PACK))
        nc.sync.dma_start(raw[1][:], w2.rearrange("(p j) c -> p j c", j=PACK))
        l1, l2, l3 = load_list(n1, "l_n1"), load_list(n2, "l_n2"), load_list(n3, "l_n3")
        minus = sb.tile([P, W], F32, name="minus", align_bytes=64)
        nc.gpsimd.memset(minus[:], -1.0)

        gs = [sb.tile([P, S], U8, name=f"gs{i}", align_bytes=64) for i in range(2)]
        gw = [sb.tile([P, S], U32, name=f"gw{i}", align_bytes=64) for i in range(2)]
        for i in range(2):
            nc.vector.tensor_copy(gs[i][:], xs[:].indirect(pick[i][:]))

        wq = [sb.tile([P, N], U32, name=f"wq{i}", align_bytes=64) for i in range(2)]
        wsc = [sb.tile([P, N], U8, name=f"wsc{i}", align_bytes=64) for i in range(2)]

        def deal(i, u, tag, on_scalar):
            stage = sb.tile([P, 2 * P * PACK], BF16, name=f"wb{i}{u}", tag=tag, align_bytes=64)
            dst = stage[:].rearrange("p (t m j) -> p m j t", t=2, j=PACK)
            src = raw[i][:].rearrange("p j (m t) -> p m j t", t=PACK)[:, :, :, 2 * u : 2 * u + 2]
            if on_scalar:
                nc.scalar.activation(dst, src, COPY)
            else:
                nc.vector.tensor_copy(dst, src)
            return stage

        def quantise_w(i, u, stage, c0, c1):
            cols = slice(2 * P * u + c0, 2 * P * u + c1)
            nc.vector.quantize_mx(
                out=wq[i][:, cols].bitcast(FP8X4), scales=wsc[i][:, cols], in_=stage[:, PACK * c0 : PACK * c1]
            )

        for i in range(2):
            nc.vector.tensor_copy(gw[i][:], xw[:].indirect(pick[i][:]))
        quantise_w(0, 0, deal(0, 0, "first", True), 0, 2 * P)
        late = deal(0, 1, "second", True)
        stage = deal(1, 0, "first", False)
        quantise_w(1, 0, stage, 0, P)
        quantise_w(1, 0, stage, P, 2 * P)
        quantise_w(0, 1, late, 0, 2 * P)
        quantise_w(1, 1, deal(1, 1, "third", True), 0, 2 * P)

        halves = [slice(0, W), slice(W, S)]
        spans = [halves] + [[slice(0, S)]] * (PACK - 1)
        bank_tags = [["bank0", "bank1"], ["bank2"], ["bank0"], ["bank1"]]
        acc = []

        def multiply(t):
            cols = slice(t * P, (t + 1) * P)
            banks = []
            for tag, c in zip(bank_tags[t], spans[t]):
                bank = ps.tile([P, c.stop - c.start], F32, name=f"acc{t}_{c.start}", tag=tag)
                banks.append(bank)
                for i in range(2):
                    nc.tensor.matmul_mx(
                        out=bank[:],
                        lhsT=wq[i][:, cols].bitcast(FP8X4),
                        lhsT_scale=wsc[i][:, cols],
                        rhs=gw[i][:, c].bitcast(FP8X4),
                        rhs_scale=gs[i][:, c],
                        start=(i == 0),
                        stop=(i == 1),
                    )
            acc.append(banks)

        h = [sb.tile([P, S], F32, name=f"h{t}", align_bytes=64) for t in range(PACK)]
        pa = [sb.tile([P, W], F32, name=f"pa{t}", align_bytes=64) for t in range(PACK)]
        npb = [sb.tile([P, W], F32, name=f"npb{t}", align_bytes=64) for t in range(PACK)]
        dt = [sb.tile([P, S], F32, name=f"dt{t}", align_bytes=64) for t in range(PACK)]
        far = [sb.tile([P, S], F32, name=f"far{t}", align_bytes=64) for t in range(PACK)]
        y = sb.tile([P, PACK, S], F32, name="y", align_bytes=64)
        yb = sb.tile([P, S, PACK], BF16, name="yb", align_bytes=64)
        yq = sb.tile([P, S], U32, name="yq", align_bytes=64)
        ysc = sb.tile([P, S], U8, name="ysc", align_bytes=64)
        out_rows = out_0.rearrange("(p t) c -> p t c", t=PACK)
        out_words = out_1[0].rearrange("p c r -> p (c r)").bitcast(I32)

        def put_pb(t):
            multiply(t)
            for bank, c in zip(acc[t], spans[t]):
                nc.scalar.activation(h[t][:, c], bank[:], COPY)
            nc.scalar.activation(npb[t][:], h[t][:].indirect(l2[:]), COPY, scale=-1.0)
            nc.vector.tensor_tensor(dt[t][:].indirect(l1[:]), npb[t][:], minus[:], ALU.mult)

        def put_rb(t):
            nc.scalar.activation(pa[t][:], h[t][:].indirect(l1[:]), COPY)
            nc.vector.tensor_tensor(dt[t][:].indirect(l2[:]), pa[t][:], npb[t][:], ALU.add)

        def look(t, c):
            nc.scalar.activation(far[t][:, c], dt[t][:].indirect(l3[:, c.start // 16 : c.stop // 16]), COPY)

        def larger(t, c):
            dst = y[:, t, c]
            nc.vector.scalar_tensor_tensor(dst, far[t][:, c], 0.5, dt[t][:, c], ALU.mult, ALU.max)
            nc.sync.dma_start(out_rows[:, t, c], dst)

        def round_y(c, on_scalar):
            dst = yb[:, c, :].rearrange("p (c i) t -> p c t i", i=4)
            src = y[:, :, c].rearrange("p t (c i) -> p c t i", i=4)
            if on_scalar:
                nc.scalar.activation(dst, src, COPY)
            else:
                nc.vector.tensor_copy(dst, src)

        def quantise_y(c):
            nc.vector.quantize_mx(
                out=yq[:, c].bitcast(FP8X4), scales=ysc[:, c], in_=yb[:, c, :].rearrange("p c t -> p (c t)")
            )
            nc.sync.dma_start(out_words[:, c], yq[:, c].bitcast(I32))

        def finish(t):
            for c in halves:
                look(t, c)
            larger(t, slice(0, S))

        put_pb(0)
        put_pb(1)
        put_rb(0)
        put_rb(1)
        for t in (2, 3):
            put_pb(t)
            finish(t - 2)
            put_rb(t)
        finish(2)
        for c in halves:
            look(PACK - 1, c)
        larger(PACK - 1, halves[0])
        round_y(slice(64, W), False)
        round_y(slice(0, 64), True)
        larger(PACK - 1, halves[1])
        quantise_y(halves[0])
        round_y(slice(W, W + 96), True)
        round_y(slice(W + 96, S), False)
        quantise_y(halves[1])
        for q in range(4):
            eng = nc.scalar if q % 2 else nc.sync
            eng.dma_start(out_2[0, 4 * q : 4 * q + 4, :].bitcast(I32), ysc[32 * q : 32 * q + 4, :].bitcast(I32))
